import numpy as np
import ml_dtypes


def mxq(x, axis, fmt="e4m3"):
    dtype, down = {"e4m3": (ml_dtypes.float8_e4m3fn, 7), "e5m2": (ml_dtypes.float8_e5m2, 14)}[fmt]
    v = np.moveaxis(np.asarray(x, np.float32).astype(ml_dtypes.bfloat16).astype(np.float64), axis, -1)
    blocks = v.reshape(v.shape[:-1] + (-1, 32))
    amax = np.abs(blocks).max(-1, keepdims=True)
    byte = np.maximum(np.where(amax > 0, np.frexp(amax)[1] - 1 + 127, 0) - down, 1)
    scale = np.exp2(byte - 127.0)
    codes = (blocks / scale).astype(np.float32).astype(dtype).astype(np.float64)
    return np.moveaxis((codes * scale).reshape(v.shape), -1, axis)


WIDE = False


def mx_kscale(k):
    if not WIDE:
        return np.ones(k)
    levels = np.array([10, -10, 5, -5, 0])
    if k % 512:
        return np.exp2(np.random.permutation(np.resize(levels, k // 32))).repeat(32)
    a = np.empty((k // 512, 16))
    for p in range(k // 512):
        a[p, :8] = np.random.permutation(np.resize(levels, 8))
        for g in range(8):
            far = levels[np.abs(levels - a[p, g]) >= 10]
            a[p, g + 8] = far[np.random.randint(len(far))]
    return np.exp2(a.ravel()).repeat(32)


def f64(x):
    return np.asarray(x).astype(np.float64)


def striped(idx):
    return np.tile(idx.reshape(-1, 16).T, (8, 1)).astype(np.uint16)


def unstriped(offs):
    return offs[:16].T.reshape(-1).astype(np.int64)


def pack_weight(w):
    k, n = w.shape
    w = f64(np.asarray(w, np.float32).astype(ml_dtypes.bfloat16)).reshape(k // 32, 32, n)
    amax = np.abs(w).max(1)
    byte = np.clip(np.where(amax > 0, np.frexp(amax)[1] - 1 + 127 - 7, 1), 1, 254)
    scaled = (w * np.exp2(127.0 - byte)[:, None, :]).reshape(k, n).astype(np.float32)
    words = np.ascontiguousarray(scaled.reshape(k // 512, 128, 4, n).transpose(0, 1, 3, 2)).astype(ml_dtypes.float8_e4m3fn).view(np.uint8)
    return words, np.ascontiguousarray(byte.astype(np.uint8).reshape(k // 512, 16, n))


def unpack_weight(words, scales):
    g, p, n, _ = words.shape
    vals = np.ascontiguousarray(words).view(ml_dtypes.float8_e4m3fn).astype(np.float64) * np.repeat(np.exp2(scales.astype(np.float64) - 127.0), 8, axis=1)[..., None]
    return vals.transpose(0, 1, 3, 2).reshape(g * 512, n)


K, T, S, N, V = 1024, 2048, 512, 256, 256
P = 2 ** 7


def setup_inputs():
    n = np.random.standard_normal
    s = mx_kscale(K)[:, None]
    near = np.random.permutation(S)
    packed_xT = pack_weight(n((K, T)) * s)
    return {
        "x_words": packed_xT[0],
        "x_scales": packed_xT[1],
        "w1": (n((K, N)) / np.sqrt(K) / s).astype(np.float32),
        "beta": (np.tile(np.random.uniform(0.2, 1.5, S), (P, 1))).astype(np.float32),
        "pmax": (np.tile(np.random.uniform(0.7, 1.0, V), (P, 1))).astype(np.float32),
        "cpl": (np.random.uniform(0.05, 0.3, (N, 1))).astype(np.float32),
        "offs": striped(np.random.permutation(T)[:S]),
        "ra": striped(near[:V]),
        "rb": striped(near[V:]),
    }


def reference(x_words, x_scales, w1, beta, pmax, cpl, offs, ra, rb):
    xq = unpack_weight(x_words, x_scales)[:, unstriped(offs)]
    y = mxq(f64(w1), 0, "e4m3").T @ xq
    ener = (y) ** 2 + 0.5 * np.abs(y)
    ea = ener[:, unstriped(ra)]
    eb = ener[:, unstriped(rb)]
    dlt = (f64(beta)[:1][:, unstriped(ra)] - (f64(beta)[:1][:, unstriped(rb)])) * (ea - eb)
    pacc = np.minimum(np.exp(dlt), f64(pmax)[:1])
    return ea + pacc * (eb - ea) - (f64(cpl) * ((dlt) ** 2))

import concourse.mybir as mybir
from concourse.masks import make_identity

K, T, S, N, V = 1024, 2048, 512, 256, 256
FLOPS = 2 * K * N * S

F32 = mybir.dt.float32
BF16 = mybir.dt.bfloat16
I32 = mybir.dt.int32
U32 = mybir.dt.uint32
U16 = mybir.dt.uint16
U8 = mybir.dt.uint8
FP8X4 = mybir.dt.float8_e4m3fn_x4
ALU = mybir.AluOpType
ACT = mybir.ActivationFunctionType

P = 128
PACK = 4
K_PASS = P * PACK
PASSES = K // K_PASS
M_TILES = N // P
HALF = S // 2
LIST_COL = 16


def tile_picked_ytempr_mix_p_kernel(tc, x_words, x_scales, w1, beta, pmax, cpl, offs, ra, rb, out):
    nc = tc.nc
    with (
        tc.tile_pool(name="lists", bufs=1) as lists,
        tc.tile_pool(name="sb", bufs=1) as sb,
        tc.psum_pool(name="psum", bufs=1) as psum,
    ):
        offs_sb = lists.tile([P, S // LIST_COL], U16, name="offs_sb")
        ra_sb = lists.tile([P, V // LIST_COL], U16, name="ra_sb")
        rb_sb = lists.tile([P, V // LIST_COL], U16, name="rb_sb")

        x_table = [sb.tile([P, T], U32, name=f"x_table{g}", align_bytes=64) for g in range(PASSES)]
        scale_table = sb.tile([P, T], U8, name="scale_table", align_bytes=64)
        w_raw = [sb.tile([P, PACK, N], F32, name=f"w_raw{g}") for g in range(PASSES)]
        beta_dealt = sb.tile([P, S // P], F32, name="beta_dealt")
        pmax_sb = sb.tile([P, V], F32, name="pmax_sb")
        cpl_sb = sb.tile([P, M_TILES], F32, name="cpl_sb")
        ident = sb.tile([P, P], F32, name="ident")

        def load_w(g):
            rows = w1[g * K_PASS : (g + 1) * K_PASS, :]
            nc.sync.dma_start(out=w_raw[g][:], in_=rows.rearrange("(p j) m -> p j m", j=PACK))

        def load_x(g):
            nc.sync.dma_start(out=x_table[g][:].bitcast(I32), in_=x_words[g].rearrange("p n t -> p (n t)").bitcast(I32))

        def load_scales():
            for q in range(4):
                nc.sync.dma_start(
                    out=scale_table[32 * q : 32 * q + 4 * PASSES, :].bitcast(I32),
                    in_=x_scales[:, 4 * q : 4 * q + 4, :].bitcast(I32),
                )

        nc.vector.memset(scale_table[:].bitcast(I32), 0)
        nc.scalar.dma_start(out=beta_dealt[:], in_=beta[0, :].rearrange("(p j) -> p j", p=P))
        make_identity(nc, ident[:])

        load_w(0)
        load_w(1)
        nc.sync.dma_start(offs_sb[:], offs)
        load_scales()
        load_x(0)
        nc.sync.dma_start(ra_sb[:], ra)
        nc.sync.dma_start(rb_sb[:], rb)
        load_x(1)
        nc.sync.dma_start(out=pmax_sb[:], in_=pmax)
        with nc.allow_non_contiguous_dma(reason="one weight a partition"):
            nc.sync.dma_start(out=cpl_sb[:], in_=cpl.rearrange("(t p) o -> p (t o)", p=P))

        beta_ps = psum.tile([P, S // P, P], F32, name="beta_ps")
        for j in range(S // P):
            nc.tensor.transpose(beta_ps[:, j, :], beta_dealt[:, j : j + 1].to_broadcast([P, P]), ident[:])
        beta_row = sb.tile([P, S], F32, name="beta_row")
        nc.scalar.copy(out=beta_row[:].rearrange("p (c j) -> p c j", j=S // P), in_=beta_ps[:].rearrange("p j c -> p c j"))

        w_codes = [sb.tile([P, N], U32, name=f"w_codes{g}", align_bytes=64) for g in range(PASSES)]
        w_scales = [sb.tile([P, N], U8, name=f"w_scales{g}", align_bytes=64) for g in range(PASSES)]
        for g in range(PASSES):
            grouped = sb.tile([P, N, PACK], BF16, name=f"grouped{g}", align_bytes=64)
            nc.scalar.copy(
                out=grouped[:].rearrange("p (c i) j -> p c j i", i=4),
                in_=w_raw[g][:].rearrange("p j (c i) -> p c j i", i=4),
            )
            nc.vector.quantize_mx(
                out=w_codes[g][:].bitcast(FP8X4),
                scales=w_scales[g][:],
                in_=grouped[:].rearrange("p m j -> p (m j)"),
            )

        x_scale = sb.tile([P, S], U8, name="x_scale", align_bytes=64)
        x_first = sb.tile([P, S], U32, name="x_first", align_bytes=64)
        beta_a = sb.tile([P, V], F32, name="beta_a")
        beta_gap = sb.tile([P, V], F32, name="beta_gap")

        def gather_scales():
            nc.vector.tensor_copy(x_scale[:], scale_table[:].indirect(offs_sb[:]))

        def gather_first():
            nc.vector.tensor_copy(x_first[:], x_table[0][:].indirect(offs_sb[:]))

        def gather_beta():
            nc.vector.tensor_copy(beta_a[:], beta_row[:].indirect(ra_sb[:]))
            nc.vector.tensor_tensor(beta_gap[:], beta_row[:].indirect(rb_sb[:]), beta_a[:], ALU.subtract)

        gather_scales()
        gather_first()
        gather_beta()

        x_last = [sb.tile([P, HALF], U32, name=f"x_last{h}", align_bytes=64) for h in range(2)]
        half_cols = HALF // LIST_COL
        for h in range(2):
            nc.vector.tensor_copy(x_last[h][:], x_table[1][:].indirect(offs_sb[:, h * half_cols : (h + 1) * half_cols]))

        y = [[psum.tile([P, HALF], F32, name=f"y{t}{h}") for h in range(2)] for t in range(M_TILES)]
        for g in range(PASSES):
            for h in range(2):
                cols = slice(h * HALF, (h + 1) * HALF)
                moving = x_first[:, cols] if g == 0 else x_last[h][:]
                for t in range(M_TILES):
                    rows = slice(t * P, (t + 1) * P)
                    nc.tensor.matmul_mx(
                        out=y[t][h][:],
                        lhsT=w_codes[g][:, rows].bitcast(FP8X4),
                        lhsT_scale=w_scales[g][:, rows],
                        rhs=moving.bitcast(FP8X4),
                        rhs_scale=x_scale[4 * g : P, cols],
                        start=(g == 0),
                        stop=(g == PASSES - 1),
                    )

        def tiles(name, width):
            return [sb.tile([P, width], F32, name=f"{name}{t}") for t in range(M_TILES)]

        ener = tiles("ener", S)
        ea, gap, dlt, chance, square = (tiles(name, V) for name in ("ea", "gap", "dlt", "chance", "square"))
        pacc, rest, moved, result = (tiles(name, V) for name in ("pacc", "rest", "moved", "result"))

        def energy(t, h):
            size = sb.tile([P, HALF], F32, name=f"size{t}{h}")
            nc.scalar.activation(size[:], y[t][h][:], ACT.Abs)
            nc.vector.scalar_tensor_tensor(ener[t][:, h * HALF : (h + 1) * HALF], size[:], 0.5, size[:], ALU.add, ALU.mult)

        def fetch_first(t):
            nc.vector.tensor_copy(ea[t][:], ener[t][:].indirect(ra_sb[:]))

        def fetch_gap(t):
            nc.vector.tensor_tensor(gap[t][:], ener[t][:].indirect(rb_sb[:]), ea[t][:], ALU.subtract)

        def exponent(t):
            nc.vector.tensor_tensor(dlt[t][:], gap[t][:], beta_gap[:], ALU.mult)
            nc.scalar.activation(chance[t][:], dlt[t][:], ACT.Exp)
            nc.scalar.activation(square[t][:], dlt[t][:], ACT.Square)

        def cap(t):
            nc.vector.tensor_tensor(pacc[t][:], chance[t][:], pmax_sb[:], ALU.min)

        def penalty(t):
            nc.vector.scalar_tensor_tensor(rest[t][:], square[t][:], cpl_sb[:, t : t + 1], ea[t][:], ALU.mult, ALU.subtract)

        def move(t):
            nc.vector.tensor_tensor(moved[t][:], pacc[t][:], gap[t][:], ALU.mult)

        def finish(t):
            nc.vector.tensor_tensor(result[t][:], moved[t][:], rest[t][:], ALU.subtract)
            nc.sync.dma_start(out=out[t * P : (t + 1) * P, :], in_=result[t][:])

        energy(0, 0)
        energy(1, 0)
        energy(0, 1)
        steps = [lambda t: energy(t, 1), fetch_first, fetch_gap, exponent, cap, penalty, move, finish]
        for i in range(1, len(steps) + 1):
            if i < len(steps):
                steps[i](0)
            steps[i - 1](1)
